import numpy as np
import ml_dtypes


def mxq(x, axis, fmt="e4m3"):
    dtype, down = {"e4m3": (ml_dtypes.float8_e4m3fn, 7), "e5m2": (ml_dtypes.float8_e5m2, 14)}[fmt]
    v = np.moveaxis(np.asarray(x, np.float32).astype(ml_dtypes.bfloat16).astype(np.float64), axis, -1)
    blocks = v.reshape(v.shape[:-1] + (-1, 32))
    amax = np.abs(blocks).max(-1, keepdims=True)
    byte = np.maximum(np.where(amax > 0, np.frexp(amax)[1] - 1 + 127, 0) - down, 1)
    scale = np.exp2(byte - 127.0)
    codes = (blocks / scale).astype(np.float32).astype(dtype).astype(np.float64)
    return np.moveaxis((codes * scale).reshape(v.shape), -1, axis)


WIDE = False


def mx_kscale(k):
    if not WIDE:
        return np.ones(k)
    levels = np.array([10, -10, 5, -5, 0])
    if k % 512:
        return np.exp2(np.random.permutation(np.resize(levels, k // 32))).repeat(32)
    a = np.empty((k // 512, 16))
    for p in range(k // 512):
        a[p, :8] = np.random.permutation(np.resize(levels, 8))
        for g in range(8):
            far = levels[np.abs(levels - a[p, g]) >= 10]
            a[p, g + 8] = far[np.random.randint(len(far))]
    return np.exp2(a.ravel()).repeat(32)


def f64(x):
    return np.asarray(x).astype(np.float64)


def striped(idx):
    return np.tile(idx.reshape(-1, 16).T, (8, 1)).astype(np.uint16)


def unstriped(offs):
    return offs[:16].T.reshape(-1).astype(np.int64)


def gelu(v):
    return 0.5 * v * (1.0 + np.tanh(np.sqrt(2.0 / np.pi) * (v + 0.044715 * v**3)))


K, T, E, C, H, N = 1024, 1536, 4, 256, 512, 256


def by_expert(wq, xq):
    return np.concatenate([wq[e].T @ xq[:, e * C:(e + 1) * C] for e in range(E)], axis=1)


def setup_inputs():
    n = np.random.standard_normal
    s = mx_kscale(K)[:, None]
    u = mx_kscale(H)
    return {
        "xT": (n((K, T)) * s).astype(np.float32),
        "xr": n((N, T)).astype(np.float32),
        "w1": (n((E, K, H)) / np.sqrt(K) / s[None]).astype(np.float32),
        "w3": (n((E, K, H)) / np.sqrt(K) / s[None] * u[None, None, :]).astype(np.float32),
        "w2": (n((E, H, N)) / np.sqrt(H) / u[None, :, None]).astype(np.float32),
        "gate": np.tile(np.random.uniform(0.2, 1.0, E * C), (N, 1)).astype(np.float32),
        "offs": striped(np.random.permutation(T)[:E * C]),
    }


def reference(xT, xr, w1, w3, w2, gate, offs):
    idx = unstriped(offs)
    xq = mxq(f64(xT)[:, idx], 0, "e4m3")
    h = gelu(by_expert(mxq(f64(w1), 1, "e4m3"), xq))
    h = h * by_expert(mxq(f64(w3), 1, "e4m3"), xq)
    y = by_expert(mxq(f64(w2), 1, "e4m3"), mxq(h, 0, "e4m3"))
    out = f64(xr).copy()
    out[:, idx] += f64(gate) * y
    return out

@@ -1,0 +1,167 @@
+import concourse.mybir as mybir
+
+K, T, E, C, H, N = 1024, 1536, 4, 256, 512, 256
+FLOPS = 2 * E * C * (2 * K * H + H * N)
+BYTES = 4 * (K * T + N * T + 2 * E * K * H + E * H * N + E * C + N * T) + 2 * 128 * E * C // 16
+
+F32 = mybir.dt.float32
+BF16 = mybir.dt.bfloat16
+U32 = mybir.dt.uint32
+U16 = mybir.dt.uint16
+U8 = mybir.dt.uint8
+FP8X4 = mybir.dt.float8_e4m3fn_x4
+MULT, ADD = mybir.AluOpType.mult, mybir.AluOpType.add
+GELU = mybir.ActivationFunctionType.Gelu_apprx_tanh
+
+P = 128
+PASSES = K // 512
+TC = 512
+TOK_V = 256
+W_V = 0
+W_V_LAST = 80
+W2_V = 0
+W2_V_LAST = 176
+
+
+def tile_moe_res_glu_gelu_kernel(tc, xT, xr, w1, w3, w2, gate, offs, out):
+    nc = tc.nc
+    with (
+        tc.tile_pool(name="held", bufs=1) as held,
+        tc.tile_pool(name="rawp", bufs=9) as rawp,
+        tc.tile_pool(name="grp", bufs=4) as grp,
+        tc.tile_pool(name="codes", bufs=3) as codes,
+        tc.tile_pool(name="work", bufs=3) as work,
+        tc.psum_pool(name="psum", bufs=1) as psum,
+    ):
+        offsets = held.tile([P, E * C // 16], U16, name="offsets")
+        warm = held.tile([P, 8], F32, name="warm")
+        tok_words = [held.tile([P, T], U32, name=f"tok_words{s}", align_bytes=64) for s in range(PASSES)]
+        tok_bytes = held.tile([P, T], U8, name="tok_bytes", align_bytes=64)
+        gate_sb = held.tile([P, E * C], F32, name="gate_sb")
+        win = [held.tile([P, T], F32, name=f"win{b}") for b in range(2)]
+        xr_sb = [held.tile([P, T], F32, name=f"xr_sb{b}") for b in range(2)]
+        out_sb = [held.tile([P, T], F32, name=f"out_sb{b}") for b in range(2)]
+
+        nc.gpsimd.memset(tok_bytes[:], 0)
+        nc.vector.memset(warm[:], 0.0)
+        for b in range(2):
+            nc.vector.memset(win[b][:], 0.0)
+        nc.scalar.activation(warm[:], warm[:], GELU)
+
+        first = True
+        for s in range(PASSES):
+            for c in range(T // TC):
+                raw = rawp.tile([P, 4, TC], F32, name="raw")
+                nc.sync.dma_start(raw[:], xT[s * 512 : (s + 1) * 512, c * TC : (c + 1) * TC].rearrange("(p j) t -> p j t", j=4))
+                if first:
+                    nc.sync.dma_start(offsets[:], offs)
+                    first = False
+                grouped = grp.tile([P, TC, 4], BF16, name="tok_grouped", tag="grouped", align_bytes=64)
+                dst = grouped[:].rearrange("p (c i) j -> p c j i", i=4)
+                src = raw[:].rearrange("p j (c i) -> p c j i", i=4)
+                cut = TOK_V // 4
+                nc.vector.tensor_copy(dst[:, :cut], src[:, :cut])
+                nc.scalar.copy(dst[:, cut:], src[:, cut:])
+                nc.vector.quantize_mx(
+                    out=tok_words[s][:, c * TC : (c + 1) * TC].bitcast(FP8X4),
+                    scales=tok_bytes[4 * s : P, c * TC : (c + 1) * TC],
+                    in_=grouped[:].rearrange("p t j -> p (t j)"),
+                )
+
+        def expand(w, e, s, name, m_v):
+            raw = rawp.tile([P, 4, H], F32, name="raw")
+            nc.sync.dma_start(raw[:], w[e, s * 512 : (s + 1) * 512, :].rearrange("(p j) c -> p j c", j=4))
+            grouped = grp.tile([P, 4, 128, 4], BF16, name="w_grouped", tag="grouped", align_bytes=64)
+            dst = grouped[:].rearrange("p t m j -> p m j t")
+            src = raw[:].rearrange("p j (m t) -> p m j t", t=4)
+            if m_v:
+                nc.vector.tensor_copy(dst[:, :m_v], src[:, :m_v])
+            nc.scalar.copy(dst[:, m_v:], src[:, m_v:])
+            words = codes.tile([P, H], U32, name=f"{name}_words{s}", align_bytes=64)
+            scales = codes.tile([P, H], U8, name=f"{name}_scales{s}", align_bytes=64)
+            nc.vector.quantize_mx(out=words[:].bitcast(FP8X4), scales=scales[:], in_=grouped[:].rearrange("p t m j -> p (t m j)"))
+            return words, scales
+
+        for e in range(E):
+            last = e == E - 1
+            g_words = []
+            for s in range(PASSES):
+                gw = work.tile([P, C], U32, name=f"g_words{s}", align_bytes=64)
+                nc.vector.tensor_copy(gw[:], tok_words[s][:].indirect(offsets[:, e * 16 : (e + 1) * 16]))
+                g_words.append(gw)
+            g_bytes = work.tile([P, C], U8, name="g_bytes", align_bytes=64)
+            nc.vector.tensor_copy(g_bytes[:], tok_bytes[:].indirect(offsets[:, e * 16 : (e + 1) * 16]))
+
+            w1q = [expand(w1, e, s, "w1", W_V) for s in range(PASSES)]
+            w3q = [expand(w3, e, s, "w3", W_V_LAST if last and s == 1 else W_V) for s in range(PASSES)]
+
+            raw2 = held.tile([P, 4, N], F32, name=f"raw2_{e}")
+            nc.sync.dma_start(raw2[:], w2[e].rearrange("(p j) n -> p j n", j=4))
+            grouped2 = grp.tile([P, N, 4], BF16, name="w2_grouped", bufs=2, align_bytes=64)
+            dst = grouped2[:].rearrange("p (c i) j -> p c j i", i=4)
+            src = raw2[:].rearrange("p j (c i) -> p c j i", i=4)
+            cut = (W2_V_LAST if last else W2_V) // 4
+            if cut:
+                nc.vector.tensor_copy(dst[:, :cut], src[:, :cut])
+            nc.scalar.copy(dst[:, cut:], src[:, cut:])
+            w2_words = codes.tile([P, N], U32, name="w2_words", align_bytes=64)
+            w2_scales = codes.tile([P, N], U8, name="w2_scales", align_bytes=64)
+            nc.vector.quantize_mx(out=w2_words[:].bitcast(FP8X4), scales=w2_scales[:], in_=grouped2[:].rearrange("p n j -> p (n j)"))
+
+            if e == 0:
+                nc.sync.dma_start(gate_sb[:], gate[0:P, :])
+            if last:
+                for b in range(2):
+                    nc.sync.dma_start(xr_sb[b][:], xr[b * P : (b + 1) * P, :])
+
+            def first_layer(wq, bank, cols):
+                for t in range(4):
+                    for s in range(PASSES):
+                        words, scales = wq[s]
+                        nc.tensor.matmul_mx(
+                            out=bank[:, t, :],
+                            lhsT=words[:, t * 128 : (t + 1) * 128].bitcast(FP8X4),
+                            lhsT_scale=scales[:, t * 128 : (t + 1) * 128],
+                            rhs=g_words[s][:, cols].bitcast(FP8X4),
+                            rhs_scale=g_bytes[4 * s : P, cols],
+                            start=s == 0,
+                            stop=s == PASSES - 1,
+                        )
+
+            y = psum.tile([P, 2, C], F32, name="y", bufs=2)
+            gelus = []
+            for half in range(2):
+                cols = slice(half * 128, (half + 1) * 128)
+                a = psum.tile([P, 4, 128], F32, name="a", bufs=3)
+                first_layer(w1q, a, cols)
+                ga = work.tile([P, 128, 4], F32, name="ga")
+                nc.scalar.activation(ga[:], a[:].rearrange("p t n -> p n t"), GELU)
+                gelus.append(ga)
+            for half in range(2):
+                cols = slice(half * 128, (half + 1) * 128)
+                b3 = psum.tile([P, 4, 128], F32, name="b3", bufs=3)
+                first_layer(w3q, b3, cols)
+                h = work.tile([P, 128, 4], BF16, name="h", align_bytes=64)
+                nc.vector.tensor_tensor(h[:], b3[:].rearrange("p t n -> p n t"), gelus[half][:], MULT)
+                h_words = work.tile([P, 128], U32, name="h_words", align_bytes=64)
+                h_scales = work.tile([P, 128], U8, name="h_scales", align_bytes=64)
+                nc.vector.quantize_mx(out=h_words[:].bitcast(FP8X4), scales=h_scales[:], in_=h[:].rearrange("p n t -> p (n t)"))
+                for b in range(2):
+                    nc.tensor.matmul_mx(
+                        out=y[:, b, cols],
+                        lhsT=w2_words[:, b * 128 : (b + 1) * 128].bitcast(FP8X4),
+                        lhsT_scale=w2_scales[:, b * 128 : (b + 1) * 128],
+                        rhs=h_words[:].bitcast(FP8X4),
+                        rhs_scale=h_scales[:],
+                        start=True,
+                        stop=True,
+                    )
+            yg = work.tile([P, 2, C], F32, name="yg")
+            for b in range(2):
+                nc.vector.tensor_tensor(yg[:, b, :], y[:, b, :], gate_sb[:, e * C : (e + 1) * C], MULT)
+                nc.vector.tensor_copy(win[b][:].indirect(offsets[:, e * 16 : (e + 1) * 16]), yg[:, b, :])
+                if last:
+                    for c in range(T // TC):
+                        cols = slice(c * TC, (c + 1) * TC)
+                        nc.vector.tensor_tensor(out_sb[b][:, cols], win[b][:, cols], xr_sb[b][:, cols], ADD)
+                        nc.sync.dma_start(out[b * P : (b + 1) * P, cols], out_sb[b][:, cols])

@@ -16,152 +16,275 @@ GELU = mybir.ActivationFunctionType.Gelu_apprx_tanh
 P = 128
 PASSES = K // 512
 TC = 512
-TOK_V = 256
-W_V = 0
-W_V_LAST = 80
-W2_V = 0
-W2_V_LAST = 176
+V_SHARE = {("w1", 0, 1): 40, ("w3", 0, 1): 40, ("w1", 1, 1): 40, ("w3", 1, 1): 40, ("w1", 2, 1): 40, ("w3", 2, 1): 40, ("w1", 3, 1): 40, ("w3", 3, 1): 64}
+SINGLE = (("w3", 3),)
+LOOKAHEAD = 8
 
 
 def tile_moe_res_glu_gelu_kernel(tc, xT, xr, w1, w3, w2, gate, offs, out):
     nc = tc.nc
     with (
         tc.tile_pool(name="held", bufs=1) as held,
-        tc.tile_pool(name="rawp", bufs=9) as rawp,
-        tc.tile_pool(name="grp", bufs=4) as grp,
-        tc.tile_pool(name="codes", bufs=3) as codes,
-        tc.tile_pool(name="work", bufs=3) as work,
+        tc.tile_pool(name="rawp", bufs=11) as rawp,
+        tc.tile_pool(name="grp", bufs=3) as grp,
+        tc.tile_pool(name="codes", bufs=2) as codes,
+        tc.tile_pool(name="work", bufs=2) as work,
         tc.psum_pool(name="psum", bufs=1) as psum,
     ):
         offsets = held.tile([P, E * C // 16], U16, name="offsets")
         warm = held.tile([P, 8], F32, name="warm")
         tok_words = [held.tile([P, T], U32, name=f"tok_words{s}", align_bytes=64) for s in range(PASSES)]
         tok_bytes = held.tile([P, T], U8, name="tok_bytes", align_bytes=64)
-        gate_sb = held.tile([P, E * C], F32, name="gate_sb")
         win = [held.tile([P, T], F32, name=f"win{b}") for b in range(2)]
-        xr_sb = [held.tile([P, T], F32, name=f"xr_sb{b}") for b in range(2)]
+        late = {}
         out_sb = [held.tile([P, T], F32, name=f"out_sb{b}") for b in range(2)]
 
+        chunks = [("x", 0, s, c) for s in range(PASSES) for c in range(T // TC)]
+        for e in range(E):
+            chunks += [("w1", e, 0, 0), ("w1", e, 1, 0), ("w3", e, 0, 0)]
+            chunks += [("w2", e, 0, 0), ("w3", e, 1, 0)] if e < E - 1 else [("w3", e, 1, 0), ("w2", e, 0, 0)]
+        raws, groups, weights = {}, {}, {}
+        first_layer_in = {"w1": w1, "w3": w3}
+
+        def load(i):
+            kind, e, s, c = chunks[i]
+            if kind == "x":
+                raw = rawp.tile([P, 4, TC], F32, name="raw")
+                nc.sync.dma_start(raw[:], xT[s * 512 : (s + 1) * 512, c * TC : (c + 1) * TC].rearrange("(p j) t -> p j t", j=4))
+            elif kind == "w2":
+                raw = rawp.tile([P, 4, N], F32, name="raw2", tag="raw")
+                nc.sync.dma_start(raw[:], w2[e].rearrange("(p j) n -> p j n", j=4))
+            else:
+                raw = rawp.tile([P, 4, H], F32, name="raw")
+                nc.sync.dma_start(raw[:], first_layer_in[kind][e, s * 512 : (s + 1) * 512, :].rearrange("(p j) c -> p j c", j=4))
+            raws[i] = raw
+            if i == 0:
+                nc.sync.dma_start(offsets[:], offs)
+            if chunks[i] == ("w3", 1, 0, 0):
+                late["gate"] = grp.tile([P, E * C], F32, name="gate_sb", tag="tok_grouped", align_bytes=64)
+                nc.sync.dma_start(late["gate"][:], gate[0:P, :])
+            if i == len(chunks) - 1:
+                for b in range(2):
+                    late[b] = rawp.tile([P, T], F32, name=f"xr_sb{b}", tag="raw")
+                    nc.sync.dma_start(late[b][:], xr[b * P : (b + 1) * P, :])
+
+        def share(dst, src, cut, whole):
+            if cut:
+                nc.vector.tensor_copy(dst[:, :cut], src[:, :cut])
+            if cut < whole:
+                nc.scalar.copy(dst[:, cut:], src[:, cut:])
+
+        def interleave(i):
+            kind, e, s, c = chunks[i]
+            raw = raws.pop(i)
+            if kind == "x":
+                grouped = grp.tile([P, TC, 4], BF16, name="tok_grouped", align_bytes=64)
+                share(grouped[:].rearrange("p (c i) j -> p c j i", i=4), raw[:].rearrange("p j (c i) -> p c j i", i=4), 128 // 4, TC // 4)
+            elif kind == "w2":
+                grouped = grp.tile([P, N, 4], BF16, name="w2_grouped", bufs=2, align_bytes=64)
+                share(grouped[:].rearrange("p (c i) j -> p c j i", i=4), raw[:].rearrange("p j (c i) -> p c j i", i=4), 256 // 4, N // 4)
+            else:
+                if s == 0:
+                    groups[kind, e] = grp.tile([P, 2, 4, 128, 4], BF16, name="w_grouped", align_bytes=64)
+                grouped = groups[kind, e][:, s]
+                m_v = V_SHARE.get(chunks[i][:3], 0)
+                share(grouped.rearrange("p t m j -> p m j t"), raw[:].rearrange("p j (m t) -> p m j t", t=4), m_v, 128)
+            groups[i] = grouped
+
+        def quantize(i):
+            kind, e, s, c = chunks[i]
+            grouped = groups.pop(i)
+            if kind == "x":
+                nc.vector.quantize_mx(
+                    out=tok_words[s][:, c * TC : (c + 1) * TC].bitcast(FP8X4),
+                    scales=tok_bytes[4 * s : P, c * TC : (c + 1) * TC],
+                    in_=grouped[:].rearrange("p t j -> p (t j)"),
+                )
+                return
+            if kind == "w2":
+                words = codes.tile([P, N], U32, name="w2_words", align_bytes=64)
+                scales = codes.tile([P, N], U8, name="w2_scales", align_bytes=64)
+                flat = grouped[:].rearrange("p n j -> p (n j)")
+            else:
+                if (kind, e) not in weights:
+                    words = codes.tile([P, PASSES * H], U32, name=f"{kind}_words", align_bytes=64)
+                    scales = codes.tile([P, PASSES * H], U8, name=f"{kind}_scales", align_bytes=64)
+                    weights[kind, e] = (words, scales)
+                both = groups[kind, e]
+                if (kind, e) in SINGLE:
+                    words, scales = (t[:, s * H : (s + 1) * H] for t in weights[kind, e])
+                    nc.vector.quantize_mx(out=words.bitcast(FP8X4), scales=scales, in_=both[:, s].rearrange("p t m j -> p (t m j)"))
+                else:
+                    words, scales = weights[kind, e]
+                    nc.vector.quantize_mx(out=words[:].bitcast(FP8X4), scales=scales[:], in_=both[:].rearrange("p s t m j -> p (s t m j)"))
+                return
+            nc.vector.quantize_mx(out=words[:].bitcast(FP8X4), scales=scales[:], in_=flat)
+            weights[kind, e] = (words, scales)
+
+        gathered, banks, gelus, hidden, ys, ygs = {}, {}, {}, {}, {}, {}
+
+        def idx(e, n=1):
+            return offsets[:, e * 16 : (e + n) * 16]
+
+        def gather_words(es, s):
+            gw = work.tile([P, len(es) * C], U32, name=f"g_words{s}_{es[0]}", bufs=1, align_bytes=64)
+            nc.vector.tensor_copy(gw[:], tok_words[s][:].indirect(idx(es[0], len(es))))
+            for q, e in enumerate(es):
+                gathered[e, s] = gw, q * C
+
+        def gather_bytes(es):
+            gb = work.tile([P, len(es) * C], U8, name=f"g_bytes_{es[0]}", bufs=1, align_bytes=64)
+            nc.vector.tensor_copy(gb[:], tok_bytes[:].indirect(idx(es[0], len(es))))
+            for q, e in enumerate(es):
+                gathered[e, "bytes"] = gb
+
+        def first_layer(kind, e, half):
+            bank = psum.tile([P, 4, 128], F32, name=f"bank_{kind}", bufs=3)
+            for t in range(4):
+                for s in range(PASSES):
+                    words, scales = weights[kind, e]
+                    m_cols = slice(s * H + t * 128, s * H + (t + 1) * 128)
+                    gw, first = gathered[e, s]
+                    cols = slice(first + half * 128, first + (half + 1) * 128)
+                    nc.tensor.matmul_mx(
+                        out=bank[:, t, :],
+                        lhsT=words[:, m_cols].bitcast(FP8X4),
+                        lhsT_scale=scales[:, m_cols],
+                        rhs=gw[:, cols].bitcast(FP8X4),
+                        rhs_scale=gathered[e, "bytes"][4 * s : P, cols],
+                        start=s == 0,
+                        stop=s == PASSES - 1,
+                    )
+            banks[kind, half] = bank
+
+        def gelu(half):
+            ga = work.tile([P, 128, 4], F32, name="ga", bufs=3)
+            nc.scalar.activation(ga[:], banks["w1", half][:].rearrange("p t n -> p n t"), GELU)
+            gelus[half] = ga
+
+        def product(half):
+            if half == 0:
+                hidden["h"] = work.tile([P, C, 4], BF16, name="h", align_bytes=64)
+            nc.vector.tensor_tensor(
+                hidden["h"][:, half * 128 : (half + 1) * 128, :], banks["w3", half][:].rearrange("p t n -> p n t"), gelus[half][:], MULT
+            )
+
+        def second_layer(e, first, n):
+            if first == 0:
+                hidden["q"] = (
+                    work.tile([P, C], U32, name="h_words", align_bytes=64),
+                    work.tile([P, C], U8, name="h_scales", align_bytes=64),
+                )
+                ys[e] = psum.tile([P, 2, C], F32, name="y", bufs=2)
+            cols = slice(first, first + n)
+            h_words, h_scales = hidden["q"]
+            nc.vector.quantize_mx(out=h_words[:, cols].bitcast(FP8X4), scales=h_scales[:, cols], in_=hidden["h"][:, cols, :].rearrange("p n t -> p (n t)"))
+            words, scales = weights["w2", e]
+            for b in range(2):
+                nc.tensor.matmul_mx(
+                    out=ys[e][:, b, cols],
+                    lhsT=words[:, b * 128 : (b + 1) * 128].bitcast(FP8X4),
+                    lhsT_scale=scales[:, b * 128 : (b + 1) * 128],
+                    rhs=h_words[:, cols].bitcast(FP8X4),
+                    rhs_scale=h_scales[:, cols],
+                    start=True,
+                    stop=True,
+                )
+
+        def weigh(e, blocks):
+            for b in blocks:
+                yg = work.tile([P, C], F32, name=f"yg{b}")
+                nc.vector.tensor_tensor(yg[:], ys[e][:, b, :], late["gate"][:, e * C : (e + 1) * C], MULT)
+                ygs[e, b] = yg
+
+        def scatter(e, b):
+            nc.vector.tensor_copy(win[b][:].indirect(idx(e)), ygs[e, b][:])
+
+        def finish(b, engines):
+            cuts = (0, 1024, 1536)
+            for engine, c0, c1 in zip(engines, cuts[:-1], cuts[1:]):
+                cols = slice(c0, c1)
+                engine.tensor_tensor(out_sb[b][:, cols], win[b][:, cols], late[b][:, cols], ADD)
+                nc.sync.dma_start(out[b * P : (b + 1) * P, cols], out_sb[b][:, cols])
+
+        for i in range(LOOKAHEAD):
+            load(i)
         nc.gpsimd.memset(tok_bytes[:], 0)
         nc.vector.memset(warm[:], 0.0)
         for b in range(2):
             nc.vector.memset(win[b][:], 0.0)
         nc.scalar.activation(warm[:], warm[:], GELU)
 
-        first = True
-        for s in range(PASSES):
-            for c in range(T // TC):
-                raw = rawp.tile([P, 4, TC], F32, name="raw")
-                nc.sync.dma_start(raw[:], xT[s * 512 : (s + 1) * 512, c * TC : (c + 1) * TC].rearrange("(p j) t -> p j t", j=4))
-                if first:
-                    nc.sync.dma_start(offsets[:], offs)
-                    first = False
-                grouped = grp.tile([P, TC, 4], BF16, name="tok_grouped", tag="grouped", align_bytes=64)
-                dst = grouped[:].rearrange("p (c i) j -> p c j i", i=4)
-                src = raw[:].rearrange("p j (c i) -> p c j i", i=4)
-                cut = TOK_V // 4
-                nc.vector.tensor_copy(dst[:, :cut], src[:, :cut])
-                nc.scalar.copy(dst[:, cut:], src[:, cut:])
-                nc.vector.quantize_mx(
-                    out=tok_words[s][:, c * TC : (c + 1) * TC].bitcast(FP8X4),
-                    scales=tok_bytes[4 * s : P, c * TC : (c + 1) * TC],
-                    in_=grouped[:].rearrange("p t j -> p (t j)"),
-                )
+        pos = {c: i for i, c in enumerate(chunks)}
 
-        def expand(w, e, s, name, m_v):
-            raw = rawp.tile([P, 4, H], F32, name="raw")
-            nc.sync.dma_start(raw[:], w[e, s * 512 : (s + 1) * 512, :].rearrange("(p j) c -> p j c", j=4))
-            grouped = grp.tile([P, 4, 128, 4], BF16, name="w_grouped", tag="grouped", align_bytes=64)
-            dst = grouped[:].rearrange("p t m j -> p m j t")
-            src = raw[:].rearrange("p j (m t) -> p m j t", t=4)
-            if m_v:
-                nc.vector.tensor_copy(dst[:, :m_v], src[:, :m_v])
-            nc.scalar.copy(dst[:, m_v:], src[:, m_v:])
-            words = codes.tile([P, H], U32, name=f"{name}_words{s}", align_bytes=64)
-            scales = codes.tile([P, H], U8, name=f"{name}_scales{s}", align_bytes=64)
-            nc.vector.quantize_mx(out=words[:].bitcast(FP8X4), scales=scales[:], in_=grouped[:].rearrange("p t m j -> p (t m j)"))
-            return words, scales
+        def X(kind, e, s=0, c=0):
+            i = pos[kind, e, s, c]
+            interleave(i)
+            if i + LOOKAHEAD < len(chunks):
+                load(i + LOOKAHEAD)
 
-        for e in range(E):
+        def Q(kind, e, s=1, c=0):
+            quantize(pos[kind, e, s, c])
+
+        for i in range(6):
+            X("x", 0, i // 3, i % 3)
+            if i > 0:
+                Q("x", 0, (i - 1) // 3, (i - 1) % 3)
+            if i == 4:
+                gather_words((0,), 0)
+        X("w1", 0, 0)
+        Q("x", 0, 1, 2)
+        gather_words((0,), 1)
+        gather_bytes((0,))
+        X("w1", 0, 1)
+        gather_words((1, 2, 3), 0)
+        Q("w1", 0)
+        first_layer("w1", 0, 0)
+        first_layer("w1", 0, 1)
+        X("w3", 0, 0)
+        gather_words((1, 2, 3), 1)
+        X("w2", 0)
+        X("w3", 0, 1)
+        gelu(0)
+        gelu(1)
+        Q("w3", 0)
+        first_layer("w3", 0, 0)
+        first_layer("w3", 0, 1)
+        gather_bytes((1, 2, 3))
+        for e in range(1, E):
             last = e == E - 1
-            g_words = []
-            for s in range(PASSES):
-                gw = work.tile([P, C], U32, name=f"g_words{s}", align_bytes=64)
-                nc.vector.tensor_copy(gw[:], tok_words[s][:].indirect(offsets[:, e * 16 : (e + 1) * 16]))
-                g_words.append(gw)
-            g_bytes = work.tile([P, C], U8, name="g_bytes", align_bytes=64)
-            nc.vector.tensor_copy(g_bytes[:], tok_bytes[:].indirect(offsets[:, e * 16 : (e + 1) * 16]))
-
-            w1q = [expand(w1, e, s, "w1", W_V) for s in range(PASSES)]
-            w3q = [expand(w3, e, s, "w3", W_V_LAST if last and s == 1 else W_V) for s in range(PASSES)]
-
-            raw2 = held.tile([P, 4, N], F32, name=f"raw2_{e}")
-            nc.sync.dma_start(raw2[:], w2[e].rearrange("(p j) n -> p j n", j=4))
-            grouped2 = grp.tile([P, N, 4], BF16, name="w2_grouped", bufs=2, align_bytes=64)
-            dst = grouped2[:].rearrange("p (c i) j -> p c j i", i=4)
-            src = raw2[:].rearrange("p j (c i) -> p c j i", i=4)
-            cut = (W2_V_LAST if last else W2_V) // 4
-            if cut:
-                nc.vector.tensor_copy(dst[:, :cut], src[:, :cut])
-            nc.scalar.copy(dst[:, cut:], src[:, cut:])
-            w2_words = codes.tile([P, N], U32, name="w2_words", align_bytes=64)
-            w2_scales = codes.tile([P, N], U8, name="w2_scales", align_bytes=64)
-            nc.vector.quantize_mx(out=w2_words[:].bitcast(FP8X4), scales=w2_scales[:], in_=grouped2[:].rearrange("p n j -> p (n j)"))
-
-            if e == 0:
-                nc.sync.dma_start(gate_sb[:], gate[0:P, :])
-            if last:
-                for b in range(2):
-                    nc.sync.dma_start(xr_sb[b][:], xr[b * P : (b + 1) * P, :])
-
-            def first_layer(wq, bank, cols):
-                for t in range(4):
-                    for s in range(PASSES):
-                        words, scales = wq[s]
-                        nc.tensor.matmul_mx(
-                            out=bank[:, t, :],
-                            lhsT=words[:, t * 128 : (t + 1) * 128].bitcast(FP8X4),
-                            lhsT_scale=scales[:, t * 128 : (t + 1) * 128],
-                            rhs=g_words[s][:, cols].bitcast(FP8X4),
-                            rhs_scale=g_bytes[4 * s : P, cols],
-                            start=s == 0,
-                            stop=s == PASSES - 1,
-                        )
-
-            y = psum.tile([P, 2, C], F32, name="y", bufs=2)
-            gelus = []
-            for half in range(2):
-                cols = slice(half * 128, (half + 1) * 128)
-                a = psum.tile([P, 4, 128], F32, name="a", bufs=3)
-                first_layer(w1q, a, cols)
-                ga = work.tile([P, 128, 4], F32, name="ga")
-                nc.scalar.activation(ga[:], a[:].rearrange("p t n -> p n t"), GELU)
-                gelus.append(ga)
-            for half in range(2):
-                cols = slice(half * 128, (half + 1) * 128)
-                b3 = psum.tile([P, 4, 128], F32, name="b3", bufs=3)
-                first_layer(w3q, b3, cols)
-                h = work.tile([P, 128, 4], BF16, name="h", align_bytes=64)
-                nc.vector.tensor_tensor(h[:], b3[:].rearrange("p t n -> p n t"), gelus[half][:], MULT)
-                h_words = work.tile([P, 128], U32, name="h_words", align_bytes=64)
-                h_scales = work.tile([P, 128], U8, name="h_scales", align_bytes=64)
-                nc.vector.quantize_mx(out=h_words[:].bitcast(FP8X4), scales=h_scales[:], in_=h[:].rearrange("p n t -> p (n t)"))
-                for b in range(2):
-                    nc.tensor.matmul_mx(
-                        out=y[:, b, cols],
-                        lhsT=w2_words[:, b * 128 : (b + 1) * 128].bitcast(FP8X4),
-                        lhsT_scale=w2_scales[:, b * 128 : (b + 1) * 128],
-                        rhs=h_words[:].bitcast(FP8X4),
-                        rhs_scale=h_scales[:],
-                        start=True,
-                        stop=True,
-                    )
-            yg = work.tile([P, 2, C], F32, name="yg")
-            for b in range(2):
-                nc.vector.tensor_tensor(yg[:, b, :], y[:, b, :], gate_sb[:, e * C : (e + 1) * C], MULT)
-                nc.vector.tensor_copy(win[b][:].indirect(offsets[:, e * 16 : (e + 1) * 16]), yg[:, b, :])
-                if last:
-                    for c in range(T // TC):
-                        cols = slice(c * TC, (c + 1) * TC)
-                        nc.vector.tensor_tensor(out_sb[b][:, cols], win[b][:, cols], xr_sb[b][:, cols], ADD)
-                        nc.sync.dma_start(out[b * P : (b + 1) * P, cols], out_sb[b][:, cols])
+            X("w1", e, 0)
+            if e > 1:
+                scatter(e - 2, 1)
+            product(0)
+            product(1)
+            Q("w2", e - 1, 0)
+            second_layer(e - 1, 0, C)
+            X("w1", e, 1)
+            Q("w1", e)
+            first_layer("w1", e, 0)
+            first_layer("w1", e, 1)
+            X("w3", e, 0)
+            weigh(e - 1, (0, 1))
+            if e < E - 1:
+                X("w2", e)
+            scatter(e - 1, 0)
+            if ("w3", e) in SINGLE:
+                Q("w3", e, 0)
+            X("w3", e, 1)
+            gelu(0)
+            gelu(1)
+            Q("w3", e)
+            first_layer("w3", e, 0)
+            first_layer("w3", e, 1)
+        X("w2", E - 1)
+        scatter(E - 2, 1)
+        product(0)
+        product(1)
+        Q("w2", E - 1, 0)
+        second_layer(E - 1, 0, C)
+        weigh(E - 1, (0, 1))
+        for b in range(2):
+            scatter(E - 1, b)
+        finish(0, (nc.vector, nc.vector))
+        finish(1, (nc.vector, nc.vector))

import concourse.mybir as mybir

K, T, E, C, H, N = 1024, 1536, 4, 256, 512, 256
FLOPS = 2 * E * C * (2 * K * H + H * N)
BYTES = 4 * (K * T + N * T + 2 * E * K * H + E * H * N + E * C + N * T) + 2 * 128 * E * C // 16

F32 = mybir.dt.float32
BF16 = mybir.dt.bfloat16
U32 = mybir.dt.uint32
U16 = mybir.dt.uint16
U8 = mybir.dt.uint8
FP8X4 = mybir.dt.float8_e4m3fn_x4
MULT, ADD = mybir.AluOpType.mult, mybir.AluOpType.add
GELU = mybir.ActivationFunctionType.Gelu_apprx_tanh

P = 128
PASSES = K // 512
TC = 512
V_SHARE = {("w1", 0, 1): 40, ("w3", 0, 1): 40, ("w1", 1, 1): 40, ("w3", 1, 1): 40, ("w1", 2, 1): 40, ("w3", 2, 1): 40, ("w1", 3, 1): 40, ("w3", 3, 1): 64}
SINGLE = (("w3", 3),)
LOOKAHEAD = 8


def tile_moe_res_glu_gelu_kernel(tc, xT, xr, w1, w3, w2, gate, offs, out):
    nc = tc.nc
    with (
        tc.tile_pool(name="held", bufs=1) as held,
        tc.tile_pool(name="rawp", bufs=11) as rawp,
        tc.tile_pool(name="grp", bufs=3) as grp,
        tc.tile_pool(name="codes", bufs=2) as codes,
        tc.tile_pool(name="work", bufs=2) as work,
        tc.psum_pool(name="psum", bufs=1) as psum,
    ):
        offsets = held.tile([P, E * C // 16], U16, name="offsets")
        warm = held.tile([P, 8], F32, name="warm")
        tok_words = [held.tile([P, T], U32, name=f"tok_words{s}", align_bytes=64) for s in range(PASSES)]
        tok_bytes = held.tile([P, T], U8, name="tok_bytes", align_bytes=64)
        win = [held.tile([P, T], F32, name=f"win{b}") for b in range(2)]
        late = {}
        out_sb = [held.tile([P, T], F32, name=f"out_sb{b}") for b in range(2)]

        chunks = [("x", 0, s, c) for s in range(PASSES) for c in range(T // TC)]
        for e in range(E):
            chunks += [("w1", e, 0, 0), ("w1", e, 1, 0), ("w3", e, 0, 0)]
            chunks += [("w2", e, 0, 0), ("w3", e, 1, 0)] if e < E - 1 else [("w3", e, 1, 0), ("w2", e, 0, 0)]
        raws, groups, weights = {}, {}, {}
        first_layer_in = {"w1": w1, "w3": w3}

        def load(i):
            kind, e, s, c = chunks[i]
            if kind == "x":
                raw = rawp.tile([P, 4, TC], F32, name="raw")
                nc.sync.dma_start(raw[:], xT[s * 512 : (s + 1) * 512, c * TC : (c + 1) * TC].rearrange("(p j) t -> p j t", j=4))
            elif kind == "w2":
                raw = rawp.tile([P, 4, N], F32, name="raw2", tag="raw")
                nc.sync.dma_start(raw[:], w2[e].rearrange("(p j) n -> p j n", j=4))
            else:
                raw = rawp.tile([P, 4, H], F32, name="raw")
                nc.sync.dma_start(raw[:], first_layer_in[kind][e, s * 512 : (s + 1) * 512, :].rearrange("(p j) c -> p j c", j=4))
            raws[i] = raw
            if i == 0:
                nc.sync.dma_start(offsets[:], offs)
            if chunks[i] == ("w3", 1, 0, 0):
                late["gate"] = grp.tile([P, E * C], F32, name="gate_sb", tag="tok_grouped", align_bytes=64)
                nc.sync.dma_start(late["gate"][:], gate[0:P, :])
            if i == len(chunks) - 1:
                for b in range(2):
                    late[b] = rawp.tile([P, T], F32, name=f"xr_sb{b}", tag="raw")
                    nc.sync.dma_start(late[b][:], xr[b * P : (b + 1) * P, :])

        def share(dst, src, cut, whole):
            if cut:
                nc.vector.tensor_copy(dst[:, :cut], src[:, :cut])
            if cut < whole:
                nc.scalar.copy(dst[:, cut:], src[:, cut:])

        def interleave(i):
            kind, e, s, c = chunks[i]
            raw = raws.pop(i)
            if kind == "x":
                grouped = grp.tile([P, TC, 4], BF16, name="tok_grouped", align_bytes=64)
                share(grouped[:].rearrange("p (c i) j -> p c j i", i=4), raw[:].rearrange("p j (c i) -> p c j i", i=4), 128 // 4, TC // 4)
            elif kind == "w2":
                grouped = grp.tile([P, N, 4], BF16, name="w2_grouped", bufs=2, align_bytes=64)
                share(grouped[:].rearrange("p (c i) j -> p c j i", i=4), raw[:].rearrange("p j (c i) -> p c j i", i=4), 256 // 4, N // 4)
            else:
                if s == 0:
                    groups[kind, e] = grp.tile([P, 2, 4, 128, 4], BF16, name="w_grouped", align_bytes=64)
                grouped = groups[kind, e][:, s]
                m_v = V_SHARE.get(chunks[i][:3], 0)
                share(grouped.rearrange("p t m j -> p m j t"), raw[:].rearrange("p j (m t) -> p m j t", t=4), m_v, 128)
            groups[i] = grouped

        def quantize(i):
            kind, e, s, c = chunks[i]
            grouped = groups.pop(i)
            if kind == "x":
                nc.vector.quantize_mx(
                    out=tok_words[s][:, c * TC : (c + 1) * TC].bitcast(FP8X4),
                    scales=tok_bytes[4 * s : P, c * TC : (c + 1) * TC],
                    in_=grouped[:].rearrange("p t j -> p (t j)"),
                )
                return
            if kind == "w2":
                words = codes.tile([P, N], U32, name="w2_words", align_bytes=64)
                scales = codes.tile([P, N], U8, name="w2_scales", align_bytes=64)
                flat = grouped[:].rearrange("p n j -> p (n j)")
            else:
                if (kind, e) not in weights:
                    words = codes.tile([P, PASSES * H], U32, name=f"{kind}_words", align_bytes=64)
                    scales = codes.tile([P, PASSES * H], U8, name=f"{kind}_scales", align_bytes=64)
                    weights[kind, e] = (words, scales)
                both = groups[kind, e]
                if (kind, e) in SINGLE:
                    words, scales = (t[:, s * H : (s + 1) * H] for t in weights[kind, e])
                    nc.vector.quantize_mx(out=words.bitcast(FP8X4), scales=scales, in_=both[:, s].rearrange("p t m j -> p (t m j)"))
                else:
                    words, scales = weights[kind, e]
                    nc.vector.quantize_mx(out=words[:].bitcast(FP8X4), scales=scales[:], in_=both[:].rearrange("p s t m j -> p (s t m j)"))
                return
            nc.vector.quantize_mx(out=words[:].bitcast(FP8X4), scales=scales[:], in_=flat)
            weights[kind, e] = (words, scales)

        gathered, banks, gelus, hidden, ys, ygs = {}, {}, {}, {}, {}, {}

        def idx(e, n=1):
            return offsets[:, e * 16 : (e + n) * 16]

        def gather_words(es, s):
            gw = work.tile([P, len(es) * C], U32, name=f"g_words{s}_{es[0]}", bufs=1, align_bytes=64)
            nc.vector.tensor_copy(gw[:], tok_words[s][:].indirect(idx(es[0], len(es))))
            for q, e in enumerate(es):
                gathered[e, s] = gw, q * C

        def gather_bytes(es):
            gb = work.tile([P, len(es) * C], U8, name=f"g_bytes_{es[0]}", bufs=1, align_bytes=64)
            nc.vector.tensor_copy(gb[:], tok_bytes[:].indirect(idx(es[0], len(es))))
            for q, e in enumerate(es):
                gathered[e, "bytes"] = gb

        def first_layer(kind, e, half):
            bank = psum.tile([P, 4, 128], F32, name=f"bank_{kind}", bufs=3)
            for t in range(4):
                for s in range(PASSES):
                    words, scales = weights[kind, e]
                    m_cols = slice(s * H + t * 128, s * H + (t + 1) * 128)
                    gw, first = gathered[e, s]
                    cols = slice(first + half * 128, first + (half + 1) * 128)
                    nc.tensor.matmul_mx(
                        out=bank[:, t, :],
                        lhsT=words[:, m_cols].bitcast(FP8X4),
                        lhsT_scale=scales[:, m_cols],
                        rhs=gw[:, cols].bitcast(FP8X4),
                        rhs_scale=gathered[e, "bytes"][4 * s : P, cols],
                        start=s == 0,
                        stop=s == PASSES - 1,
                    )
            banks[kind, half] = bank

        def gelu(half):
            ga = work.tile([P, 128, 4], F32, name="ga", bufs=3)
            nc.scalar.activation(ga[:], banks["w1", half][:].rearrange("p t n -> p n t"), GELU)
            gelus[half] = ga

        def product(half):
            if half == 0:
                hidden["h"] = work.tile([P, C, 4], BF16, name="h", align_bytes=64)
            nc.vector.tensor_tensor(
                hidden["h"][:, half * 128 : (half + 1) * 128, :], banks["w3", half][:].rearrange("p t n -> p n t"), gelus[half][:], MULT
            )

        def second_layer(e, first, n):
            if first == 0:
                hidden["q"] = (
                    work.tile([P, C], U32, name="h_words", align_bytes=64),
                    work.tile([P, C], U8, name="h_scales", align_bytes=64),
                )
                ys[e] = psum.tile([P, 2, C], F32, name="y", bufs=2)
            cols = slice(first, first + n)
            h_words, h_scales = hidden["q"]
            nc.vector.quantize_mx(out=h_words[:, cols].bitcast(FP8X4), scales=h_scales[:, cols], in_=hidden["h"][:, cols, :].rearrange("p n t -> p (n t)"))
            words, scales = weights["w2", e]
            for b in range(2):
                nc.tensor.matmul_mx(
                    out=ys[e][:, b, cols],
                    lhsT=words[:, b * 128 : (b + 1) * 128].bitcast(FP8X4),
                    lhsT_scale=scales[:, b * 128 : (b + 1) * 128],
                    rhs=h_words[:, cols].bitcast(FP8X4),
                    rhs_scale=h_scales[:, cols],
                    start=True,
                    stop=True,
                )

        def weigh(e, blocks):
            for b in blocks:
                yg = work.tile([P, C], F32, name=f"yg{b}")
                nc.vector.tensor_tensor(yg[:], ys[e][:, b, :], late["gate"][:, e * C : (e + 1) * C], MULT)
                ygs[e, b] = yg

        def scatter(e, b):
            nc.vector.tensor_copy(win[b][:].indirect(idx(e)), ygs[e, b][:])

        def finish(b, engines):
            cuts = (0, 1024, 1536)
            for engine, c0, c1 in zip(engines, cuts[:-1], cuts[1:]):
                cols = slice(c0, c1)
                engine.tensor_tensor(out_sb[b][:, cols], win[b][:, cols], late[b][:, cols], ADD)
                nc.sync.dma_start(out[b * P : (b + 1) * P, cols], out_sb[b][:, cols])

        for i in range(LOOKAHEAD):
            load(i)
        nc.gpsimd.memset(tok_bytes[:], 0)
        nc.vector.memset(warm[:], 0.0)
        for b in range(2):
            nc.vector.memset(win[b][:], 0.0)
        nc.scalar.activation(warm[:], warm[:], GELU)

        pos = {c: i for i, c in enumerate(chunks)}

        def X(kind, e, s=0, c=0):
            i = pos[kind, e, s, c]
            interleave(i)
            if i + LOOKAHEAD < len(chunks):
                load(i + LOOKAHEAD)

        def Q(kind, e, s=1, c=0):
            quantize(pos[kind, e, s, c])

        for i in range(6):
            X("x", 0, i // 3, i % 3)
            if i > 0:
                Q("x", 0, (i - 1) // 3, (i - 1) % 3)
            if i == 4:
                gather_words((0,), 0)
        X("w1", 0, 0)
        Q("x", 0, 1, 2)
        gather_words((0,), 1)
        gather_bytes((0,))
        X("w1", 0, 1)
        gather_words((1, 2, 3), 0)
        Q("w1", 0)
        first_layer("w1", 0, 0)
        first_layer("w1", 0, 1)
        X("w3", 0, 0)
        gather_words((1, 2, 3), 1)
        X("w2", 0)
        X("w3", 0, 1)
        gelu(0)
        gelu(1)
        Q("w3", 0)
        first_layer("w3", 0, 0)
        first_layer("w3", 0, 1)
        gather_bytes((1, 2, 3))
        for e in range(1, E):
            last = e == E - 1
            X("w1", e, 0)
            if e > 1:
                scatter(e - 2, 1)
            product(0)
            product(1)
            Q("w2", e - 1, 0)
            second_layer(e - 1, 0, C)
            X("w1", e, 1)
            Q("w1", e)
            first_layer("w1", e, 0)
            first_layer("w1", e, 1)
            X("w3", e, 0)
            weigh(e - 1, (0, 1))
            if e < E - 1:
                X("w2", e)
            scatter(e - 1, 0)
            if ("w3", e) in SINGLE:
                Q("w3", e, 0)
            X("w3", e, 1)
            gelu(0)
            gelu(1)
            Q("w3", e)
            first_layer("w3", e, 0)
            first_layer("w3", e, 1)
        X("w2", E - 1)
        scatter(E - 2, 1)
        product(0)
        product(1)
        Q("w2", E - 1, 0)
        second_layer(E - 1, 0, C)
        weigh(E - 1, (0, 1))
        for b in range(2):
            scatter(E - 1, b)
        finish(0, (nc.vector, nc.vector))
        finish(1, (nc.vector, nc.vector))
